import numpy as np, ml_dtypes
CORES = [40,64,80,88,96,104,120,144]
N = 8
import mx_ref
NC = 256
A = np.float32(0.03)
BF = ml_dtypes.bfloat16
def setup_inputs(rng):
    def f(*shape):
        return mx_ref.flush((rng.standard_normal(shape, dtype=np.float32) * np.exp2(rng.integers(-2, 3, shape[:-1] + (1,)))).astype(BF))
    return {"x": f(N, 128, 512), "w": f(N, 128, 4 * NC)}
def setup_inputs_blocks(rng):
    d = setup_inputs(rng)
    for k in ("x", "w"): d[k] = mx_ref.spread(d[k], rng, 2)
    return d
def setup_inputs_sharp(rng):
    d = setup_inputs(rng); d["w"] = (d["w"].astype(np.float32) * 32).astype(BF)
    return d
def setup_inputs_apart(rng):
    d = setup_inputs(rng); d["w"] = mx_ref.flush((d["w"].astype(np.float32) * np.exp2(rng.permutation(np.linspace(-3, 3, N))).astype(np.float32).reshape(N, 1, 1)).astype(BF))
    return d
def reference(x, w):
    W = [mx_ref.quantize(w[r]) for r in range(N)]
    y = np.zeros((N, 128, N * NC), np.float32)
    for j in range(N):
        X = mx_ref.quantize(x[j])
        L = [(mx_ref.matmul(X, W[r]) * A).astype(np.float64) for r in range(N)]
        m = np.max([l.max(axis=1, keepdims=True) for l in L], axis=0); s = sum(np.exp(l - m).sum(axis=1, keepdims=True) for l in L)
        for r in range(N):
            y[r][:, NC * j:NC * j + NC] = (np.exp(L[r] - m) / s).astype(np.float32)
    return {"y": y}

@@ -1,0 +1,235 @@
+import numpy as np
+from concourse.bass import DstId, RemoteDMATransfer
+from concourse.mybir import dt, AluOpType, AxisListType, ActivationFunctionType
+
+N = 8
+NC = 256
+XW = 128
+NSIM = 256
+BANK = 512
+A = float(np.float32(0.03))
+G = 4
+SL = 2 * G
+CW = N * SL
+
+SCRATCH = {
+    "xb": ("sbuf", [128, 4 * XW], "bfloat16"),
+    "wb": ("sbuf", [128, 4 * NC], "bfloat16"),
+    "xq": ("sbuf", [128, N * XW], "float8_e4m3fn_x4"),
+    "xs": ("sbuf", [128, N * XW], "uint8"),
+    "wq": ("sbuf", [128, NC], "float8_e4m3fn_x4"),
+    "ws": ("sbuf", [128, NC], "uint8"),
+    "ps": ("psum", [128, N * BANK], "float32"),
+    "e": ("sbuf", [128, N * NC], "float32"),
+    "sa": ("sbuf", [128, 2 * CW], "float32"),
+    "pq": ("sbuf", [128, 2 * CW], "float32"),
+    "qq": ("sbuf", [128, 2 * CW], "float32"),
+    "rn": ("sbuf", [128, N], "float32"),
+    "t1": ("sbuf", [128, CW], "float32"),
+    "t2": ("sbuf", [128, CW // 2], "float32"),
+    "t3": ("sbuf", [128, CW // 4], "float32"),
+    "u1": ("sbuf", [128, CW], "float32"),
+    "u2": ("sbuf", [128, CW // 2], "float32"),
+    "u3": ("sbuf", [128, CW // 4], "float32"),
+    "ri": ("sbuf", [128, 2 * G], "float32"),
+    "ff": ("sbuf", [128, 2 * G], "float32"),
+}
+SEMAPHORES = (["ldx", "ldw", "qx", "qw", "ms", "hs", "hc", "ls", "st"]
+              + ["%s%d" % (p, j) for p in ("xa", "mm", "va", "vb", "sd") for j in range(N)]
+              + ["%s%d" % (p, c) for p in ("ex", "sc", "fa", "fb", "fc", "fe", "fq", "ga", "gb", "gc", "fr", "fg")
+                 for c in range(2)])
+
+
+def _bits(m):
+    return bin(m).count("1")
+
+
+def _plan(T, topo):
+    cores = list(T.cores)
+    g0 = [j for j in range(N) if j == 0 or topo.may_write(cores[0], cores[j])]
+    groups = [g0, [j for j in range(N) if j not in g0]]
+    cls = [0 if j in g0 else 1 for j in range(N)]
+    relays = []
+    for s in range(N):
+        c = cores[s]
+        far = groups[1 - cls[s]]
+        a = groups[cls[s]].index(s)
+        own = [k for k in range(NSIM) if k != c and topo.host(k) == topo.host(c) and topo.chip(k) == topo.chip(c)
+               and all(topo.may_write(k, cores[d]) for d in far)]
+        other = [k for k in own if topo.die(k) != topo.die(c)][0]
+        same = [k for k in own if topo.die(k) == topo.die(c)][0]
+        relays.append([(other, [far[a % G], far[(a + 1) % G]]), (same, [far[(a + 2) % G], far[(a + 3) % G]])])
+    return cores, groups, cls, relays
+
+
+def _send(g, T, topo, src_core, parts, local_sem):
+    trs, tot = [], 0
+    for mask, dsts, view, sem in parts:
+        ids = []
+        for d in dsts:
+            rid, pid = topo.addr(d, src_core)
+            ids.append(DstId(rid=rid, pnc=pid))
+        trs.append(RemoteDMATransfer(dst_ids=ids, dma_engine_mask=mask, remote_sem=sem,
+                                     srcs=[view()], dsts=[view() for _ in dsts]))
+        tot += _bits(mask)
+    g.remote_dma_fused(trs, local_sem=local_sem)
+    return tot
+
+
+def _and_masks(topo, src, dsts):
+    m = topo.mask(src, dsts[0])
+    for d in dsts[1:]:
+        m &= topo.mask(src, d)
+    return m
+
+
+def _views(T, s):
+    plane = lambda: T.xs[:, s * XW:(s + 1) * XW]
+    codes = lambda: T.xq[:, s * XW:(s + 1) * XW].bitcast(dt.uint8)
+    stats = [(lambda c=c: T.sa[:, c * CW + s * SL:c * CW + (s + 1) * SL]) for c in range(2)]
+    return plane, codes, stats
+
+
+def _relay(g, core, T, topo, s, dst_ranks, cores, cls):
+    S = T.sem
+    plane, codes, stats = _views(T, s)
+    dsts = [cores[d] for d in dst_ranks]
+    mask = _and_masks(topo, core, dsts)
+    inn = _bits(topo.mask(cores[s], core) & ~_and_masks(topo, cores[s], [cores[j] for j in range(N) if j != s and cls[j] == cls[s]]))
+    tot = 0
+    g.wait_ge(S.hs, inn)
+    tot += _send(g, T, topo, core, [(mask, dsts, plane, S["xa%d" % s])], S.ls)
+    g.wait_ge(S.hc, inn)
+    tot += _send(g, T, topo, core, [(mask, dsts, codes, S["xa%d" % s])], S.ls)
+    for c in (cls[s], 1 - cls[s]):
+        g.wait_ge(S["sc%d" % c], inn)
+        tot += _send(g, T, topo, core, [(mask, dsts, stats[c], S["sc%d" % c])], S.ls)
+    g.wait_ge(S.ls, tot)
+
+
+def rank_program(g, core, T, topo):
+    cores, groups, cls, relays = _plan(T, topo)
+    r = T.rank_of(core)
+    if r is None:
+        for s in range(N):
+            for h, dst_ranks in relays[s]:
+                if h == core:
+                    _relay(g, core, T, topo, s, dst_ranks, cores, cls)
+        return
+
+    S = T.sem
+    V, ACT, PE, SY = g.vector, g.scalar, g.tensor, g.sync
+    Exp, Copy = ActivationFunctionType.Exp, ActivationFunctionType.Copy
+    mine, far = groups[cls[r]], groups[1 - cls[r]]
+    a = mine.index(r)
+    near_dst = [mine[(a + k) % G] for k in range(1, G)]
+    near_src = [mine[(a - k) % G] for k in range(1, G)]
+    far_src = [far[a % G], far[(a - 2) % G], far[(a - 1) % G], far[(a - 3) % G]]
+    order = [r] + near_src + far_src
+    lo = _and_masks(topo, core, [cores[d] for d in near_dst])
+    helpers = [h for h, _ in relays[r]]
+    hi = _and_masks(topo, core, helpers) & ~lo
+    plane, codes, stats = _views(T, r)
+
+    def blk(j):
+        return T.e[:, j * NC:(j + 1) * NC]
+
+    def bank(j):
+        return T.ps[:, j * BANK:j * BANK + NC]
+
+    def col(j, part):
+        k = cls[j] * CW + r * SL + part * G + groups[cls[j]].index(j)
+        return T.sa[:, k:k + 1]
+
+    SY.dma_start(T.xb[:], T.x[:]).then_inc(S.ldx, 16)
+    SY.dma_start(T.wb[:], T.w[:]).then_inc(S.ldw, 16)
+
+    V.memset(T.pq[:], 0.0).then_inc(S.ms, 1)
+    V.wait_ge(S.ldx, 16)
+    V.quantize_mx(T.xq[:, r * XW:(r + 1) * XW], T.xs[:, r * XW:(r + 1) * XW], T.xb[:]).then_inc(S.qx, 1)
+    V.wait_ge(S.ldw, 16)
+    V.quantize_mx(T.wq[:], T.ws[:], T.wb[:]).then_inc(S.qw, 1)
+
+    near_cores = [cores[d] for d in near_dst]
+    tot = 0
+    g.wait_ge(S.qx, 1)
+    tot += _send(g, T, topo, core, [(hi, helpers, plane, S.hs), (lo, near_cores, plane, S["xa%d" % r])], S.ls)
+    tot += _send(g, T, topo, core, [(hi, helpers, codes, S.hc), (lo, near_cores, codes, S["xa%d" % r])], S.ls)
+    for c in (cls[r], 1 - cls[r]):
+        g.wait_ge(S["ex%d" % c], G)
+        tot += _send(g, T, topo, core, [(hi, helpers, stats[c], S["sc%d" % c]),
+                                        (lo, near_cores, stats[c], S["sc%d" % c])], S.ls)
+    g.wait_ge(S.ls, tot)
+
+    PE.wait_ge(S.qx, 1)
+    PE.wait_ge(S.qw, 1)
+    ACT.wait_ge(S.ms, 1)
+    for j in order:
+        if j != r:
+            if cls[j] == cls[r]:
+                n_in = _bits(_and_masks(topo, cores[j], [cores[d] for d in mine if d != j]))
+            else:
+                hj = [(h, ds) for h, ds in relays[j] if r in ds][0]
+                n_in = _bits(_and_masks(topo, hj[0], [cores[d] for d in hj[1]]))
+            PE.wait_ge(S["xa%d" % j], 2 * n_in)
+        PE.matmul_mx(bank(j), T.xq[:, j * XW:(j + 1) * XW], T.xs[:, j * XW:(j + 1) * XW], T.wq[:], T.ws[:],
+                     True, True).then_inc(S["mm%d" % j], 1)
+        V.wait_ge(S["mm%d" % j], 1)
+        V.tensor_reduce(T.rn[:, j:j + 1], bank(j), AxisListType.X, AluOpType.max, negate=True).then_inc(S["va%d" % j], 1)
+        V.wait_ge(S["va%d" % j], 1)
+        V.tensor_scalar(col(j, 0), T.rn[:, j:j + 1], A, None, AluOpType.mult).then_inc(S["vb%d" % j], 1)
+        ACT.wait_ge(S["vb%d" % j], 1)
+        ACT.activation(blk(j), bank(j), Exp, bias=col(j, 0), scale=A, accum_out=col(j, 1)).then_inc(S["ex%d" % cls[j]], 1)
+
+    for c in (1 - cls[r], cls[r]):
+        n_sc = 0
+        for s in range(N):
+            if s == r:
+                continue
+            if cls[s] == cls[r]:
+                n_sc += _bits(_and_masks(topo, cores[s], [cores[d] for d in mine if d != s]))
+            else:
+                hs_ = [(h, ds) for h, ds in relays[s] if r in ds][0]
+                n_sc += _bits(_and_masks(topo, hs_[0], [cores[d] for d in hs_[1]]))
+        b = c * CW
+        sem = lambda p: S["%s%d" % (p, c)]
+        h1, h2, h3 = c * CW // 2, c * CW // 4, c * CW // 8
+        w1, w2, w3 = CW // 2, CW // 4, CW // 8
+        V.wait_ge(sem("sc"), n_sc)
+        V.wait_ge(sem("ex"), G)
+        V.tensor_tensor(T.t1[:, h1:h1 + w1], T.sa[:, b:b + w1], T.sa[:, b + w1:b + CW], AluOpType.min).then_inc(sem("fa"), 1)
+        V.wait_ge(sem("fa"), 1)
+        V.tensor_tensor(T.t2[:, h2:h2 + w2], T.t1[:, h1:h1 + w2], T.t1[:, h1 + w2:h1 + w1], AluOpType.min).then_inc(sem("fb"), 1)
+        V.wait_ge(sem("fb"), 1)
+        V.tensor_tensor(T.t3[:, h3:h3 + w3], T.t2[:, h2:h2 + w3], T.t2[:, h2 + w3:h2 + w2], AluOpType.min).then_inc(sem("fc"), 1)
+        ACT.wait_ge(sem("sc"), n_sc)
+        ACT.wait_ge(sem("ex"), G)
+        ACT.wait_ge(sem("fc"), 1)
+        for k in range(G):
+            ACT.activation(T.pq[:, b + G + k:b + CW:SL], T.sa[:, b + k:b + CW:SL], Exp,
+                           bias=T.t3[:, h3 + k:h3 + k + 1], scale=-1.0).then_inc(sem("fe"), 1)
+        V.wait_ge(S.ms, 1)
+        V.wait_ge(sem("fe"), G)
+        V.tensor_tensor(T.qq[:, b:b + CW], T.pq[:, b:b + CW], T.sa[:, b:b + CW], AluOpType.mult).then_inc(sem("fq"), 1)
+        V.wait_ge(sem("fq"), 1)
+        V.tensor_tensor(T.u1[:, h1:h1 + w1], T.qq[:, b:b + w1], T.qq[:, b + w1:b + CW], AluOpType.add).then_inc(sem("ga"), 1)
+        V.wait_ge(sem("ga"), 1)
+        V.tensor_tensor(T.u2[:, h2:h2 + w2], T.u1[:, h1:h1 + w2], T.u1[:, h1 + w2:h1 + w1], AluOpType.add).then_inc(sem("gb"), 1)
+        V.wait_ge(sem("gb"), 1)
+        V.tensor_tensor(T.u3[:, h3:h3 + w3], T.u2[:, h2:h2 + w3], T.u2[:, h2 + w3:h2 + w2], AluOpType.add).then_inc(sem("gc"), 1)
+        V.wait_ge(sem("gc"), 1)
+        V.reciprocal(T.ri[:, c * G:(c + 1) * G], T.u3[:, h3 + G:h3 + SL]).then_inc(sem("fr"), 1)
+        V.wait_ge(sem("fr"), 1)
+        V.tensor_tensor(T.ff[:, c * G:(c + 1) * G], T.pq[:, b + r * SL + G:b + (r + 1) * SL], T.ri[:, c * G:(c + 1) * G],
+                        AluOpType.mult).then_inc(sem("fg"), 1)
+        V.wait_ge(sem("fg"), 1)
+        ACT.wait_ge(sem("fg"), 1)
+        for k, j in enumerate(groups[c]):
+            f = T.ff[:, c * G + k:c * G + k + 1]
+            if k % 2 == 0:
+                V.tensor_scalar(blk(j), blk(j), f, None, AluOpType.mult).then_inc(S["sd%d" % j], 1)
+            else:
+                ACT.activation(blk(j), blk(j), Copy, scale=f).then_inc(S["sd%d" % j], 1)
+            SY.wait_ge(S["sd%d" % j], 1)
+            SY.dma_start(T.y[:, j * NC:(j + 1) * NC], blk(j)).then_inc(S.st, 16)
+    SY.wait_ge(S.st, 16 * N)

@@ -25,19 +25,14 @@ SCRATCH = {
     "pq": ("sbuf", [128, 2 * CW], "float32"),
     "qq": ("sbuf", [128, 2 * CW], "float32"),
     "rn": ("sbuf", [128, N], "float32"),
-    "t1": ("sbuf", [128, CW], "float32"),
-    "t2": ("sbuf", [128, CW // 2], "float32"),
-    "t3": ("sbuf", [128, CW // 4], "float32"),
-    "u1": ("sbuf", [128, CW], "float32"),
-    "u2": ("sbuf", [128, CW // 2], "float32"),
-    "u3": ("sbuf", [128, CW // 4], "float32"),
+    "nm": ("sbuf", [128, 2 * G], "float32"),
+    "su": ("sbuf", [128, 2 * G], "float32"),
     "ri": ("sbuf", [128, 2 * G], "float32"),
     "ff": ("sbuf", [128, 2 * G], "float32"),
 }
 SEMAPHORES = (["ldx", "ldw", "qx", "qw", "ms", "hs", "hc", "ls", "st"]
               + ["%s%d" % (p, j) for p in ("xa", "mm", "va", "vb", "sd") for j in range(N)]
-              + ["%s%d" % (p, c) for p in ("ex", "sc", "fa", "fb", "fc", "fe", "fq", "ga", "gb", "gc", "fr", "fg")
-                 for c in range(2)])
+              + ["%s%d" % (p, c) for p in ("ex", "sc", "fc", "fe", "fq", "gc", "fr", "fg") for c in range(2)])
 
 
 def _bits(m):
@@ -90,19 +85,25 @@ def _views(T, s):
     return plane, codes, stats
 
 
-def _relay(g, core, T, topo, s, dst_ranks, cores, cls):
+def _halves(topo, cores, cls, s, relay):
+    lo = _and_masks(topo, cores[s], [cores[j] for j in range(N) if j != s and cls[j] == cls[s]])
+    return lo & topo.mask(cores[s], relay), topo.mask(cores[s], relay) & ~lo
+
+
+def _relay(g, core, T, topo, s, dst_ranks, cores, cls, first):
     S = T.sem
     plane, codes, stats = _views(T, s)
     dsts = [cores[d] for d in dst_ranks]
     mask = _and_masks(topo, core, dsts)
-    inn = _bits(topo.mask(cores[s], core) & ~_and_masks(topo, cores[s], [cores[j] for j in range(N) if j != s and cls[j] == cls[s]]))
+    lo, hi = _halves(topo, cores, cls, s, core)
+    inn = _bits(hi)
     tot = 0
     g.wait_ge(S.hs, inn)
     tot += _send(g, T, topo, core, [(mask, dsts, plane, S["xa%d" % s])], S.ls)
     g.wait_ge(S.hc, inn)
     tot += _send(g, T, topo, core, [(mask, dsts, codes, S["xa%d" % s])], S.ls)
-    for c in (cls[s], 1 - cls[s]):
-        g.wait_ge(S["sc%d" % c], inn)
+    for w, c in enumerate((cls[s], 1 - cls[s])):
+        g.wait_ge(S["sc%d" % c], _bits(lo) if (w == 0 and first) else inn)
         tot += _send(g, T, topo, core, [(mask, dsts, stats[c], S["sc%d" % c])], S.ls)
     g.wait_ge(S.ls, tot)
 
@@ -112,9 +113,9 @@ def rank_program(g, core, T, topo):
     r = T.rank_of(core)
     if r is None:
         for s in range(N):
-            for h, dst_ranks in relays[s]:
+            for i, (h, dst_ranks) in enumerate(relays[s]):
                 if h == core:
-                    _relay(g, core, T, topo, s, dst_ranks, cores, cls)
+                    _relay(g, core, T, topo, s, dst_ranks, cores, cls, i == 0)
         return
 
     S = T.sem
@@ -155,10 +156,13 @@ def rank_program(g, core, T, topo):
     g.wait_ge(S.qx, 1)
     tot += _send(g, T, topo, core, [(hi, helpers, plane, S.hs), (lo, near_cores, plane, S["xa%d" % r])], S.ls)
     tot += _send(g, T, topo, core, [(hi, helpers, codes, S.hc), (lo, near_cores, codes, S["xa%d" % r])], S.ls)
-    for c in (cls[r], 1 - cls[r]):
+    for w, c in enumerate((cls[r], 1 - cls[r])):
         g.wait_ge(S["ex%d" % c], G)
-        tot += _send(g, T, topo, core, [(hi, helpers, stats[c], S["sc%d" % c]),
-                                        (lo, near_cores, stats[c], S["sc%d" % c])], S.ls)
+        if w == 0:
+            parts = [(hi, helpers[1:], stats[c], S["sc%d" % c]), (lo, helpers[:1] + near_cores, stats[c], S["sc%d" % c])]
+        else:
+            parts = [(hi, helpers, stats[c], S["sc%d" % c]), (lo, near_cores, stats[c], S["sc%d" % c])]
+        tot += _send(g, T, topo, core, parts, S.ls)
     g.wait_ge(S.ls, tot)
 
     PE.wait_ge(S.qx, 1)
@@ -176,11 +180,12 @@ def rank_program(g, core, T, topo):
                      True, True).then_inc(S["mm%d" % j], 1)
         V.wait_ge(S["mm%d" % j], 1)
         V.tensor_reduce(T.rn[:, j:j + 1], bank(j), AxisListType.X, AluOpType.max, negate=True).then_inc(S["va%d" % j], 1)
-        V.wait_ge(S["va%d" % j], 1)
-        V.tensor_scalar(col(j, 0), T.rn[:, j:j + 1], A, None, AluOpType.mult).then_inc(S["vb%d" % j], 1)
+        ACT.wait_ge(S["va%d" % j], 1)
+        ACT.activation(col(j, 0), T.rn[:, j:j + 1], Copy, scale=A).then_inc(S["vb%d" % j], 1)
         ACT.wait_ge(S["vb%d" % j], 1)
         ACT.activation(blk(j), bank(j), Exp, bias=col(j, 0), scale=A, accum_out=col(j, 1)).then_inc(S["ex%d" % cls[j]], 1)
 
+    n_st = [0]
     for c in (1 - cls[r], cls[r]):
         n_sc = 0
         for s in range(N):
@@ -192,44 +197,59 @@ def rank_program(g, core, T, topo):
                 hs_ = [(h, ds) for h, ds in relays[s] if r in ds][0]
                 n_sc += _bits(_and_masks(topo, hs_[0], [cores[d] for d in hs_[1]]))
         b = c * CW
+        q = c * G
         sem = lambda p: S["%s%d" % (p, c)]
-        h1, h2, h3 = c * CW // 2, c * CW // 4, c * CW // 8
-        w1, w2, w3 = CW // 2, CW // 4, CW // 8
         V.wait_ge(sem("sc"), n_sc)
         V.wait_ge(sem("ex"), G)
-        V.tensor_tensor(T.t1[:, h1:h1 + w1], T.sa[:, b:b + w1], T.sa[:, b + w1:b + CW], AluOpType.min).then_inc(sem("fa"), 1)
-        V.wait_ge(sem("fa"), 1)
-        V.tensor_tensor(T.t2[:, h2:h2 + w2], T.t1[:, h1:h1 + w2], T.t1[:, h1 + w2:h1 + w1], AluOpType.min).then_inc(sem("fb"), 1)
-        V.wait_ge(sem("fb"), 1)
-        V.tensor_tensor(T.t3[:, h3:h3 + w3], T.t2[:, h2:h2 + w3], T.t2[:, h2 + w3:h2 + w2], AluOpType.min).then_inc(sem("fc"), 1)
+        for k in range(G):
+            V.tensor_reduce(T.nm[:, q + k:q + k + 1], T.sa[:, b + k:b + CW:SL], AxisListType.X,
+                            AluOpType.min).then_inc(sem("fc"), 1)
         ACT.wait_ge(sem("sc"), n_sc)
         ACT.wait_ge(sem("ex"), G)
-        ACT.wait_ge(sem("fc"), 1)
+        ACT.wait_ge(sem("fc"), G)
         for k in range(G):
             ACT.activation(T.pq[:, b + G + k:b + CW:SL], T.sa[:, b + k:b + CW:SL], Exp,
-                           bias=T.t3[:, h3 + k:h3 + k + 1], scale=-1.0).then_inc(sem("fe"), 1)
+                           bias=T.nm[:, q + k:q + k + 1], scale=-1.0).then_inc(sem("fe"), 1)
         V.wait_ge(S.ms, 1)
         V.wait_ge(sem("fe"), G)
         V.tensor_tensor(T.qq[:, b:b + CW], T.pq[:, b:b + CW], T.sa[:, b:b + CW], AluOpType.mult).then_inc(sem("fq"), 1)
         V.wait_ge(sem("fq"), 1)
-        V.tensor_tensor(T.u1[:, h1:h1 + w1], T.qq[:, b:b + w1], T.qq[:, b + w1:b + CW], AluOpType.add).then_inc(sem("ga"), 1)
-        V.wait_ge(sem("ga"), 1)
-        V.tensor_tensor(T.u2[:, h2:h2 + w2], T.u1[:, h1:h1 + w2], T.u1[:, h1 + w2:h1 + w1], AluOpType.add).then_inc(sem("gb"), 1)
-        V.wait_ge(sem("gb"), 1)
-        V.tensor_tensor(T.u3[:, h3:h3 + w3], T.u2[:, h2:h2 + w3], T.u2[:, h2 + w3:h2 + w2], AluOpType.add).then_inc(sem("gc"), 1)
-        V.wait_ge(sem("gc"), 1)
-        V.reciprocal(T.ri[:, c * G:(c + 1) * G], T.u3[:, h3 + G:h3 + SL]).then_inc(sem("fr"), 1)
+        for k in range(G):
+            V.tensor_reduce(T.su[:, q + k:q + k + 1], T.qq[:, b + G + k:b + CW:SL], AxisListType.X,
+                            AluOpType.add).then_inc(sem("gc"), 1)
+        V.wait_ge(sem("gc"), G)
+        V.reciprocal(T.ri[:, q:q + G], T.su[:, q:q + G]).then_inc(sem("fr"), 1)
         V.wait_ge(sem("fr"), 1)
-        V.tensor_tensor(T.ff[:, c * G:(c + 1) * G], T.pq[:, b + r * SL + G:b + (r + 1) * SL], T.ri[:, c * G:(c + 1) * G],
-                        AluOpType.mult).then_inc(sem("fg"), 1)
-        V.wait_ge(sem("fg"), 1)
-        ACT.wait_ge(sem("fg"), 1)
-        for k, j in enumerate(groups[c]):
-            f = T.ff[:, c * G + k:c * G + k + 1]
-            if k % 2 == 0:
-                V.tensor_scalar(blk(j), blk(j), f, None, AluOpType.mult).then_inc(S["sd%d" % j], 1)
+        ACT.wait_ge(sem("fe"), G)
+        ACT.wait_ge(sem("fr"), 1)
+        runs = []
+        for j in sorted(groups[c]):
+            if runs and runs[-1][-1] == j - 1:
+                runs[-1].append(j)
             else:
-                ACT.activation(blk(j), blk(j), Copy, scale=f).then_inc(S["sd%d" % j], 1)
-            SY.wait_ge(S["sd%d" % j], 1)
-            SY.dma_start(T.y[:, j * NC:(j + 1) * NC], blk(j)).then_inc(S.st, 16)
-    SY.wait_ge(S.st, 16 * N)
+                runs.append([j])
+        runs.sort(key=lambda t: -len(t))
+        seq = [j for run in runs for j in run]
+        on_act = seq[1::2]
+
+        def own(k):
+            return T.pq[:, b + r * SL + G + k:b + r * SL + G + k + 1]
+
+        for j in on_act:
+            k = groups[c].index(j)
+            ACT.activation(T.ff[:, q + k:q + k + 1], own(k), Copy, scale=T.ri[:, q + k:q + k + 1]).then_inc(sem("fg"), 1)
+        ACT.wait_ge(sem("fg"), len(on_act))
+        for run in runs:
+            for j in run:
+                k = groups[c].index(j)
+                if j in on_act:
+                    ACT.activation(blk(j), blk(j), Copy, scale=T.ff[:, q + k:q + k + 1]).then_inc(S["sd%d" % j], 1)
+                else:
+                    V.tensor_scalar(blk(j), blk(j), own(k), T.ri[:, q + k:q + k + 1], AluOpType.mult,
+                                    AluOpType.mult).then_inc(S["sd%d" % j], 1)
+            for j in run:
+                SY.wait_ge(S["sd%d" % j], 1)
+            lo_c, hi_c = run[0] * NC, (run[-1] + 1) * NC
+            SY.dma_start(T.y[:, lo_c:hi_c], T.e[:, lo_c:hi_c]).then_inc(S.st, 16)
+            n_st[0] += 16
+    SY.wait_ge(S.st, n_st[0])

@@ -11,6 +11,7 @@ A = float(np.float32(0.03))
 G = 4
 SL = 2 * G
 CW = N * SL
+LOW = -1.0e29
 
 SCRATCH = {
     "xb": ("sbuf", [128, 4 * XW], "bfloat16"),
@@ -21,18 +22,18 @@ SCRATCH = {
     "ws": ("sbuf", [128, NC], "uint8"),
     "ps": ("psum", [128, N * BANK], "float32"),
     "e": ("sbuf", [128, N * NC], "float32"),
+    "on": ("sbuf", [128, NC], "float32"),
+    "rm": ("sbuf", [128, N * NC], "float32"),
     "sa": ("sbuf", [128, 2 * CW], "float32"),
     "pq": ("sbuf", [128, 2 * CW], "float32"),
     "qq": ("sbuf", [128, 2 * CW], "float32"),
-    "rn": ("sbuf", [128, N], "float32"),
     "nm": ("sbuf", [128, 2 * G], "float32"),
     "su": ("sbuf", [128, 2 * G], "float32"),
     "ri": ("sbuf", [128, 2 * G], "float32"),
-    "ff": ("sbuf", [128, 2 * G], "float32"),
 }
 SEMAPHORES = (["ldx", "ldw", "qx", "qw", "ms", "hs", "hc", "ls", "st"]
-              + ["%s%d" % (p, j) for p in ("xa", "mm", "va", "vb", "sd") for j in range(N)]
-              + ["%s%d" % (p, c) for p in ("ex", "sc", "fc", "fe", "fq", "gc", "fr", "fg") for c in range(2)])
+              + ["%s%d" % (p, j) for p in ("xa", "mm", "va", "sd") for j in range(N)]
+              + ["%s%d" % (p, c) for p in ("ex", "cp", "sc", "fc", "fe", "fq", "gc", "fr", "fg") for c in range(2)])
 
 
 def _bits(m):
@@ -142,14 +143,24 @@ def rank_program(g, core, T, topo):
         k = cls[j] * CW + r * SL + part * G + groups[cls[j]].index(j)
         return T.sa[:, k:k + 1]
 
+    def run_at(j):
+        return (cls[j] * G + groups[cls[j]].index(j)) * NC
+
     SY.dma_start(T.xb[:], T.x[:]).then_inc(S.ldx, 16)
     SY.dma_start(T.wb[:], T.w[:]).then_inc(S.ldw, 16)
 
+    n_ms = 3
     V.memset(T.pq[:], 0.0).then_inc(S.ms, 1)
+    V.memset(T.on[:, 0:NC - 4], 1.0).then_inc(S.ms, 1)
+    V.memset(T.on[:, NC - 4:NC], 1.0).then_inc(S.ms, 1)
+    V.wait_ge(S.ms, n_ms)
+    V.memset(T.on[:, NC - 1:NC], -A).then_inc(S.ms, 1)
+    n_ms += 1
     V.wait_ge(S.ldx, 16)
     V.quantize_mx(T.xq[:, r * XW:(r + 1) * XW], T.xs[:, r * XW:(r + 1) * XW], T.xb[:]).then_inc(S.qx, 1)
     V.wait_ge(S.ldw, 16)
     V.quantize_mx(T.wq[:], T.ws[:], T.wb[:]).then_inc(S.qw, 1)
+    V.wait_ge(S.ms, n_ms)
 
     near_cores = [cores[d] for d in near_dst]
     tot = 0
@@ -157,6 +168,7 @@ def rank_program(g, core, T, topo):
     tot += _send(g, T, topo, core, [(hi, helpers, plane, S.hs), (lo, near_cores, plane, S["xa%d" % r])], S.ls)
     tot += _send(g, T, topo, core, [(hi, helpers, codes, S.hc), (lo, near_cores, codes, S["xa%d" % r])], S.ls)
     for w, c in enumerate((cls[r], 1 - cls[r])):
+        g.wait_ge(S["cp%d" % c], 1)
         g.wait_ge(S["ex%d" % c], G)
         if w == 0:
             parts = [(hi, helpers[1:], stats[c], S["sc%d" % c]), (lo, helpers[:1] + near_cores, stats[c], S["sc%d" % c])]
@@ -167,8 +179,8 @@ def rank_program(g, core, T, topo):
 
     PE.wait_ge(S.qx, 1)
     PE.wait_ge(S.qw, 1)
-    ACT.wait_ge(S.ms, 1)
-    for j in order:
+    ACT.wait_ge(S.ms, n_ms)
+    for i, j in enumerate(order):
         if j != r:
             if cls[j] == cls[r]:
                 n_in = _bits(_and_masks(topo, cores[j], [cores[d] for d in mine if d != j]))
@@ -178,12 +190,19 @@ def rank_program(g, core, T, topo):
             PE.wait_ge(S["xa%d" % j], 2 * n_in)
         PE.matmul_mx(bank(j), T.xq[:, j * XW:(j + 1) * XW], T.xs[:, j * XW:(j + 1) * XW], T.wq[:], T.ws[:],
                      True, True).then_inc(S["mm%d" % j], 1)
+        p0 = run_at(j)
         V.wait_ge(S["mm%d" % j], 1)
-        V.tensor_reduce(T.rn[:, j:j + 1], bank(j), AxisListType.X, AluOpType.max, negate=True).then_inc(S["va%d" % j], 1)
+        V.tensor_tensor_scan(T.rm[:, p0:p0 + NC], bank(j), T.on[:], LOW, AluOpType.max,
+                             AluOpType.mult).then_inc(S["va%d" % j], 1)
         ACT.wait_ge(S["va%d" % j], 1)
-        ACT.activation(col(j, 0), T.rn[:, j:j + 1], Copy, scale=A).then_inc(S["vb%d" % j], 1)
-        ACT.wait_ge(S["vb%d" % j], 1)
-        ACT.activation(blk(j), bank(j), Exp, bias=col(j, 0), scale=A, accum_out=col(j, 1)).then_inc(S["ex%d" % cls[j]], 1)
+        ACT.activation(blk(j), bank(j), Exp, bias=T.rm[:, p0 + NC - 1:p0 + NC], scale=A,
+                       accum_out=col(j, 1)).then_inc(S["ex%d" % cls[j]], 1)
+        if i % G == G - 1:
+            c = cls[j]
+            for jj in groups[c]:
+                V.wait_ge(S["va%d" % jj], 1)
+            k0 = c * CW + r * SL
+            V.tensor_copy(T.sa[:, k0:k0 + G], T.rm[:, c * G * NC + NC - 1:(c + 1) * G * NC:NC]).then_inc(S["cp%d" % c], 1)
 
     n_st = [0]
     for c in (1 - cls[r], cls[r]):
@@ -201,16 +220,17 @@ def rank_program(g, core, T, topo):
         sem = lambda p: S["%s%d" % (p, c)]
         V.wait_ge(sem("sc"), n_sc)
         V.wait_ge(sem("ex"), G)
+        V.wait_ge(sem("cp"), 1)
         for k in range(G):
             V.tensor_reduce(T.nm[:, q + k:q + k + 1], T.sa[:, b + k:b + CW:SL], AxisListType.X,
                             AluOpType.min).then_inc(sem("fc"), 1)
         ACT.wait_ge(sem("sc"), n_sc)
         ACT.wait_ge(sem("ex"), G)
+        ACT.wait_ge(sem("cp"), 1)
         ACT.wait_ge(sem("fc"), G)
         for k in range(G):
             ACT.activation(T.pq[:, b + G + k:b + CW:SL], T.sa[:, b + k:b + CW:SL], Exp,
                            bias=T.nm[:, q + k:q + k + 1], scale=-1.0).then_inc(sem("fe"), 1)
-        V.wait_ge(S.ms, 1)
         V.wait_ge(sem("fe"), G)
         V.tensor_tensor(T.qq[:, b:b + CW], T.pq[:, b:b + CW], T.sa[:, b:b + CW], AluOpType.mult).then_inc(sem("fq"), 1)
         V.wait_ge(sem("fq"), 1)
@@ -220,8 +240,6 @@ def rank_program(g, core, T, topo):
         V.wait_ge(sem("gc"), G)
         V.reciprocal(T.ri[:, q:q + G], T.su[:, q:q + G]).then_inc(sem("fr"), 1)
         V.wait_ge(sem("fr"), 1)
-        ACT.wait_ge(sem("fe"), G)
-        ACT.wait_ge(sem("fr"), 1)
         runs = []
         for j in sorted(groups[c]):
             if runs and runs[-1][-1] == j - 1:
@@ -235,15 +253,16 @@ def rank_program(g, core, T, topo):
         def own(k):
             return T.pq[:, b + r * SL + G + k:b + r * SL + G + k + 1]
 
+        ACT.wait_ge(sem("fe"), G)
         for j in on_act:
-            k = groups[c].index(j)
-            ACT.activation(T.ff[:, q + k:q + k + 1], own(k), Copy, scale=T.ri[:, q + k:q + k + 1]).then_inc(sem("fg"), 1)
+            ACT.activation(blk(j), blk(j), Copy, scale=own(groups[c].index(j))).then_inc(sem("fg"), 1)
         ACT.wait_ge(sem("fg"), len(on_act))
+        ACT.wait_ge(sem("fr"), 1)
         for run in runs:
             for j in run:
                 k = groups[c].index(j)
                 if j in on_act:
-                    ACT.activation(blk(j), blk(j), Copy, scale=T.ff[:, q + k:q + k + 1]).then_inc(S["sd%d" % j], 1)
+                    ACT.activation(blk(j), blk(j), Copy, scale=T.ri[:, q + k:q + k + 1]).then_inc(S["sd%d" % j], 1)
                 else:
                     V.tensor_scalar(blk(j), blk(j), own(k), T.ri[:, q + k:q + k + 1], AluOpType.mult,
                                     AluOpType.mult).then_inc(S["sd%d" % j], 1)

@@ -205,7 +205,26 @@ def rank_program(g, core, T, topo):
             V.tensor_copy(T.sa[:, k0:k0 + G], T.rm[:, c * G * NC + NC - 1:(c + 1) * G * NC:NC]).then_inc(S["cp%d" % c], 1)
 
     n_st = [0]
-    for c in (1 - cls[r], cls[r]):
+
+    def sem(p, c):
+        return S["%s%d" % (p, c)]
+
+    def own(c, k):
+        k0 = c * CW + r * SL + G + k
+        return T.pq[:, k0:k0 + 1]
+
+    def split(c):
+        runs = []
+        for j in sorted(groups[c]):
+            if runs and runs[-1][-1] == j - 1:
+                runs[-1].append(j)
+            else:
+                runs.append([j])
+        runs.sort(key=lambda t: -len(t))
+        seq = [j for run in runs for j in run]
+        return runs, seq[1::2]
+
+    def head(c):
         n_sc = 0
         for s in range(N):
             if s == r:
@@ -215,60 +234,61 @@ def rank_program(g, core, T, topo):
             else:
                 hs_ = [(h, ds) for h, ds in relays[s] if r in ds][0]
                 n_sc += _bits(_and_masks(topo, hs_[0], [cores[d] for d in hs_[1]]))
-        b = c * CW
-        q = c * G
-        sem = lambda p: S["%s%d" % (p, c)]
-        V.wait_ge(sem("sc"), n_sc)
-        V.wait_ge(sem("ex"), G)
-        V.wait_ge(sem("cp"), 1)
+        b, q = c * CW, c * G
+        V.wait_ge(sem("sc", c), n_sc)
+        V.wait_ge(sem("ex", c), G)
+        V.wait_ge(sem("cp", c), 1)
         for k in range(G):
             V.tensor_reduce(T.nm[:, q + k:q + k + 1], T.sa[:, b + k:b + CW:SL], AxisListType.X,
-                            AluOpType.min).then_inc(sem("fc"), 1)
-        ACT.wait_ge(sem("sc"), n_sc)
-        ACT.wait_ge(sem("ex"), G)
-        ACT.wait_ge(sem("cp"), 1)
-        ACT.wait_ge(sem("fc"), G)
+                            AluOpType.min).then_inc(sem("fc", c), 1)
+        ACT.wait_ge(sem("sc", c), n_sc)
+        ACT.wait_ge(sem("ex", c), G)
+        ACT.wait_ge(sem("cp", c), 1)
+        ACT.wait_ge(sem("fc", c), G)
         for k in range(G):
             ACT.activation(T.pq[:, b + G + k:b + CW:SL], T.sa[:, b + k:b + CW:SL], Exp,
-                           bias=T.nm[:, q + k:q + k + 1], scale=-1.0).then_inc(sem("fe"), 1)
-        V.wait_ge(sem("fe"), G)
-        V.tensor_tensor(T.qq[:, b:b + CW], T.pq[:, b:b + CW], T.sa[:, b:b + CW], AluOpType.mult).then_inc(sem("fq"), 1)
-        V.wait_ge(sem("fq"), 1)
+                           bias=T.nm[:, q + k:q + k + 1], scale=-1.0).then_inc(sem("fe", c), 1)
+
+    def sums(c):
+        b, q = c * CW, c * G
+        V.wait_ge(sem("fe", c), G)
+        V.tensor_tensor(T.qq[:, b:b + CW], T.pq[:, b:b + CW], T.sa[:, b:b + CW], AluOpType.mult).then_inc(sem("fq", c), 1)
+        V.wait_ge(sem("fq", c), 1)
         for k in range(G):
             V.tensor_reduce(T.su[:, q + k:q + k + 1], T.qq[:, b + G + k:b + CW:SL], AxisListType.X,
-                            AluOpType.add).then_inc(sem("gc"), 1)
-        V.wait_ge(sem("gc"), G)
-        V.reciprocal(T.ri[:, q:q + G], T.su[:, q:q + G]).then_inc(sem("fr"), 1)
-        V.wait_ge(sem("fr"), 1)
-        runs = []
-        for j in sorted(groups[c]):
-            if runs and runs[-1][-1] == j - 1:
-                runs[-1].append(j)
-            else:
-                runs.append([j])
-        runs.sort(key=lambda t: -len(t))
-        seq = [j for run in runs for j in run]
-        on_act = seq[1::2]
-
-        def own(k):
-            return T.pq[:, b + r * SL + G + k:b + r * SL + G + k + 1]
-
-        ACT.wait_ge(sem("fe"), G)
+                            AluOpType.add).then_inc(sem("gc", c), 1)
+        V.wait_ge(sem("gc", c), G)
+        V.reciprocal(T.ri[:, q:q + G], T.su[:, q:q + G]).then_inc(sem("fr", c), 1)
+        on_act = split(c)[1]
+        ACT.wait_ge(sem("fe", c), G)
         for j in on_act:
-            ACT.activation(blk(j), blk(j), Copy, scale=own(groups[c].index(j))).then_inc(sem("fg"), 1)
-        ACT.wait_ge(sem("fg"), len(on_act))
-        ACT.wait_ge(sem("fr"), 1)
+            ACT.activation(blk(j), blk(j), Copy, scale=own(c, groups[c].index(j))).then_inc(sem("fg", c), 1)
+
+    def tail(c):
+        q = c * G
+        runs, on_act = split(c)
+        V.wait_ge(sem("fr", c), 1)
+        ACT.wait_ge(sem("fg", c), len(on_act))
+        ACT.wait_ge(sem("fr", c), 1)
         for run in runs:
             for j in run:
                 k = groups[c].index(j)
                 if j in on_act:
                     ACT.activation(blk(j), blk(j), Copy, scale=T.ri[:, q + k:q + k + 1]).then_inc(S["sd%d" % j], 1)
                 else:
-                    V.tensor_scalar(blk(j), blk(j), own(k), T.ri[:, q + k:q + k + 1], AluOpType.mult,
+                    V.tensor_scalar(blk(j), blk(j), own(c, k), T.ri[:, q + k:q + k + 1], AluOpType.mult,
                                     AluOpType.mult).then_inc(S["sd%d" % j], 1)
             for j in run:
                 SY.wait_ge(S["sd%d" % j], 1)
             lo_c, hi_c = run[0] * NC, (run[-1] + 1) * NC
             SY.dma_start(T.y[:, lo_c:hi_c], T.e[:, lo_c:hi_c]).then_inc(S.st, 16)
             n_st[0] += 16
+
+    c1, c2 = 1 - cls[r], cls[r]
+    head(c1)
+    sums(c1)
+    head(c2)
+    tail(c1)
+    sums(c2)
+    tail(c2)
     SY.wait_ge(S.st, n_st[0])

import numpy as np
from concourse.bass import DstId, RemoteDMATransfer
from concourse.mybir import dt, AluOpType, AxisListType, ActivationFunctionType

N = 8
NC = 256
XW = 128
NSIM = 256
BANK = 512
A = float(np.float32(0.03))
G = 4
SL = 2 * G
CW = N * SL
LOW = -1.0e29

SCRATCH = {
    "xb": ("sbuf", [128, 4 * XW], "bfloat16"),
    "wb": ("sbuf", [128, 4 * NC], "bfloat16"),
    "xq": ("sbuf", [128, N * XW], "float8_e4m3fn_x4"),
    "xs": ("sbuf", [128, N * XW], "uint8"),
    "wq": ("sbuf", [128, NC], "float8_e4m3fn_x4"),
    "ws": ("sbuf", [128, NC], "uint8"),
    "ps": ("psum", [128, N * BANK], "float32"),
    "e": ("sbuf", [128, N * NC], "float32"),
    "on": ("sbuf", [128, NC], "float32"),
    "rm": ("sbuf", [128, N * NC], "float32"),
    "sa": ("sbuf", [128, 2 * CW], "float32"),
    "pq": ("sbuf", [128, 2 * CW], "float32"),
    "qq": ("sbuf", [128, 2 * CW], "float32"),
    "nm": ("sbuf", [128, 2 * G], "float32"),
    "su": ("sbuf", [128, 2 * G], "float32"),
    "ri": ("sbuf", [128, 2 * G], "float32"),
}
SEMAPHORES = (["ldx", "ldw", "qx", "qw", "ms", "hs", "hc", "ls", "st"]
              + ["%s%d" % (p, j) for p in ("xa", "mm", "va", "sd") for j in range(N)]
              + ["%s%d" % (p, c) for p in ("ex", "cp", "sc", "fc", "fe", "fq", "gc", "fr", "fg") for c in range(2)])


def _bits(m):
    return bin(m).count("1")


def _plan(T, topo):
    cores = list(T.cores)
    g0 = [j for j in range(N) if j == 0 or topo.may_write(cores[0], cores[j])]
    groups = [g0, [j for j in range(N) if j not in g0]]
    cls = [0 if j in g0 else 1 for j in range(N)]
    relays = []
    for s in range(N):
        c = cores[s]
        far = groups[1 - cls[s]]
        a = groups[cls[s]].index(s)
        own = [k for k in range(NSIM) if k != c and topo.host(k) == topo.host(c) and topo.chip(k) == topo.chip(c)
               and all(topo.may_write(k, cores[d]) for d in far)]
        other = [k for k in own if topo.die(k) != topo.die(c)][0]
        same = [k for k in own if topo.die(k) == topo.die(c)][0]
        relays.append([(other, [far[a % G], far[(a + 1) % G]]), (same, [far[(a + 2) % G], far[(a + 3) % G]])])
    return cores, groups, cls, relays


def _send(g, T, topo, src_core, parts, local_sem):
    trs, tot = [], 0
    for mask, dsts, view, sem in parts:
        ids = []
        for d in dsts:
            rid, pid = topo.addr(d, src_core)
            ids.append(DstId(rid=rid, pnc=pid))
        trs.append(RemoteDMATransfer(dst_ids=ids, dma_engine_mask=mask, remote_sem=sem,
                                     srcs=[view()], dsts=[view() for _ in dsts]))
        tot += _bits(mask)
    g.remote_dma_fused(trs, local_sem=local_sem)
    return tot


def _and_masks(topo, src, dsts):
    m = topo.mask(src, dsts[0])
    for d in dsts[1:]:
        m &= topo.mask(src, d)
    return m


def _views(T, s):
    plane = lambda: T.xs[:, s * XW:(s + 1) * XW]
    codes = lambda: T.xq[:, s * XW:(s + 1) * XW].bitcast(dt.uint8)
    stats = [(lambda c=c: T.sa[:, c * CW + s * SL:c * CW + (s + 1) * SL]) for c in range(2)]
    return plane, codes, stats


def _halves(topo, cores, cls, s, relay):
    lo = _and_masks(topo, cores[s], [cores[j] for j in range(N) if j != s and cls[j] == cls[s]])
    return lo & topo.mask(cores[s], relay), topo.mask(cores[s], relay) & ~lo


def _relay(g, core, T, topo, s, dst_ranks, cores, cls, first):
    S = T.sem
    plane, codes, stats = _views(T, s)
    dsts = [cores[d] for d in dst_ranks]
    mask = _and_masks(topo, core, dsts)
    lo, hi = _halves(topo, cores, cls, s, core)
    inn = _bits(hi)
    tot = 0
    g.wait_ge(S.hs, inn)
    tot += _send(g, T, topo, core, [(mask, dsts, plane, S["xa%d" % s])], S.ls)
    g.wait_ge(S.hc, inn)
    tot += _send(g, T, topo, core, [(mask, dsts, codes, S["xa%d" % s])], S.ls)
    for w, c in enumerate((cls[s], 1 - cls[s])):
        g.wait_ge(S["sc%d" % c], _bits(lo) if (w == 0 and first) else inn)
        tot += _send(g, T, topo, core, [(mask, dsts, stats[c], S["sc%d" % c])], S.ls)
    g.wait_ge(S.ls, tot)


def rank_program(g, core, T, topo):
    cores, groups, cls, relays = _plan(T, topo)
    r = T.rank_of(core)
    if r is None:
        for s in range(N):
            for i, (h, dst_ranks) in enumerate(relays[s]):
                if h == core:
                    _relay(g, core, T, topo, s, dst_ranks, cores, cls, i == 0)
        return

    S = T.sem
    V, ACT, PE, SY = g.vector, g.scalar, g.tensor, g.sync
    Exp, Copy = ActivationFunctionType.Exp, ActivationFunctionType.Copy
    mine, far = groups[cls[r]], groups[1 - cls[r]]
    a = mine.index(r)
    near_dst = [mine[(a + k) % G] for k in range(1, G)]
    near_src = [mine[(a - k) % G] for k in range(1, G)]
    far_src = [far[a % G], far[(a - 2) % G], far[(a - 1) % G], far[(a - 3) % G]]
    order = [r] + near_src + far_src
    lo = _and_masks(topo, core, [cores[d] for d in near_dst])
    helpers = [h for h, _ in relays[r]]
    hi = _and_masks(topo, core, helpers) & ~lo
    plane, codes, stats = _views(T, r)

    def blk(j):
        return T.e[:, j * NC:(j + 1) * NC]

    def bank(j):
        return T.ps[:, j * BANK:j * BANK + NC]

    def col(j, part):
        k = cls[j] * CW + r * SL + part * G + groups[cls[j]].index(j)
        return T.sa[:, k:k + 1]

    def run_at(j):
        return (cls[j] * G + groups[cls[j]].index(j)) * NC

    SY.dma_start(T.xb[:], T.x[:]).then_inc(S.ldx, 16)
    SY.dma_start(T.wb[:], T.w[:]).then_inc(S.ldw, 16)

    n_ms = 3
    V.memset(T.pq[:], 0.0).then_inc(S.ms, 1)
    V.memset(T.on[:, 0:NC - 4], 1.0).then_inc(S.ms, 1)
    V.memset(T.on[:, NC - 4:NC], 1.0).then_inc(S.ms, 1)
    V.wait_ge(S.ms, n_ms)
    V.memset(T.on[:, NC - 1:NC], -A).then_inc(S.ms, 1)
    n_ms += 1
    V.wait_ge(S.ldx, 16)
    V.quantize_mx(T.xq[:, r * XW:(r + 1) * XW], T.xs[:, r * XW:(r + 1) * XW], T.xb[:]).then_inc(S.qx, 1)
    V.wait_ge(S.ldw, 16)
    V.quantize_mx(T.wq[:], T.ws[:], T.wb[:]).then_inc(S.qw, 1)
    V.wait_ge(S.ms, n_ms)

    near_cores = [cores[d] for d in near_dst]
    tot = 0
    g.wait_ge(S.qx, 1)
    tot += _send(g, T, topo, core, [(hi, helpers, plane, S.hs), (lo, near_cores, plane, S["xa%d" % r])], S.ls)
    tot += _send(g, T, topo, core, [(hi, helpers, codes, S.hc), (lo, near_cores, codes, S["xa%d" % r])], S.ls)
    for w, c in enumerate((cls[r], 1 - cls[r])):
        g.wait_ge(S["cp%d" % c], 1)
        g.wait_ge(S["ex%d" % c], G)
        if w == 0:
            parts = [(hi, helpers[1:], stats[c], S["sc%d" % c]), (lo, helpers[:1] + near_cores, stats[c], S["sc%d" % c])]
        else:
            parts = [(hi, helpers, stats[c], S["sc%d" % c]), (lo, near_cores, stats[c], S["sc%d" % c])]
        tot += _send(g, T, topo, core, parts, S.ls)
    g.wait_ge(S.ls, tot)

    PE.wait_ge(S.qx, 1)
    PE.wait_ge(S.qw, 1)
    ACT.wait_ge(S.ms, n_ms)
    for i, j in enumerate(order):
        if j != r:
            if cls[j] == cls[r]:
                n_in = _bits(_and_masks(topo, cores[j], [cores[d] for d in mine if d != j]))
            else:
                hj = [(h, ds) for h, ds in relays[j] if r in ds][0]
                n_in = _bits(_and_masks(topo, hj[0], [cores[d] for d in hj[1]]))
            PE.wait_ge(S["xa%d" % j], 2 * n_in)
        PE.matmul_mx(bank(j), T.xq[:, j * XW:(j + 1) * XW], T.xs[:, j * XW:(j + 1) * XW], T.wq[:], T.ws[:],
                     True, True).then_inc(S["mm%d" % j], 1)
        p0 = run_at(j)
        V.wait_ge(S["mm%d" % j], 1)
        V.tensor_tensor_scan(T.rm[:, p0:p0 + NC], bank(j), T.on[:], LOW, AluOpType.max,
                             AluOpType.mult).then_inc(S["va%d" % j], 1)
        ACT.wait_ge(S["va%d" % j], 1)
        ACT.activation(blk(j), bank(j), Exp, bias=T.rm[:, p0 + NC - 1:p0 + NC], scale=A,
                       accum_out=col(j, 1)).then_inc(S["ex%d" % cls[j]], 1)
        if i % G == G - 1:
            c = cls[j]
            for jj in groups[c]:
                V.wait_ge(S["va%d" % jj], 1)
            k0 = c * CW + r * SL
            V.tensor_copy(T.sa[:, k0:k0 + G], T.rm[:, c * G * NC + NC - 1:(c + 1) * G * NC:NC]).then_inc(S["cp%d" % c], 1)

    n_st = [0]

    def sem(p, c):
        return S["%s%d" % (p, c)]

    def own(c, k):
        k0 = c * CW + r * SL + G + k
        return T.pq[:, k0:k0 + 1]

    def split(c):
        runs = []
        for j in sorted(groups[c]):
            if runs and runs[-1][-1] == j - 1:
                runs[-1].append(j)
            else:
                runs.append([j])
        runs.sort(key=lambda t: -len(t))
        seq = [j for run in runs for j in run]
        return runs, seq[1::2]

    def head(c):
        n_sc = 0
        for s in range(N):
            if s == r:
                continue
            if cls[s] == cls[r]:
                n_sc += _bits(_and_masks(topo, cores[s], [cores[d] for d in mine if d != s]))
            else:
                hs_ = [(h, ds) for h, ds in relays[s] if r in ds][0]
                n_sc += _bits(_and_masks(topo, hs_[0], [cores[d] for d in hs_[1]]))
        b, q = c * CW, c * G
        V.wait_ge(sem("sc", c), n_sc)
        V.wait_ge(sem("ex", c), G)
        V.wait_ge(sem("cp", c), 1)
        for k in range(G):
            V.tensor_reduce(T.nm[:, q + k:q + k + 1], T.sa[:, b + k:b + CW:SL], AxisListType.X,
                            AluOpType.min).then_inc(sem("fc", c), 1)
        ACT.wait_ge(sem("sc", c), n_sc)
        ACT.wait_ge(sem("ex", c), G)
        ACT.wait_ge(sem("cp", c), 1)
        ACT.wait_ge(sem("fc", c), G)
        for k in range(G):
            ACT.activation(T.pq[:, b + G + k:b + CW:SL], T.sa[:, b + k:b + CW:SL], Exp,
                           bias=T.nm[:, q + k:q + k + 1], scale=-1.0).then_inc(sem("fe", c), 1)

    def sums(c):
        b, q = c * CW, c * G
        V.wait_ge(sem("fe", c), G)
        V.tensor_tensor(T.qq[:, b:b + CW], T.pq[:, b:b + CW], T.sa[:, b:b + CW], AluOpType.mult).then_inc(sem("fq", c), 1)
        V.wait_ge(sem("fq", c), 1)
        for k in range(G):
            V.tensor_reduce(T.su[:, q + k:q + k + 1], T.qq[:, b + G + k:b + CW:SL], AxisListType.X,
                            AluOpType.add).then_inc(sem("gc", c), 1)
        V.wait_ge(sem("gc", c), G)
        V.reciprocal(T.ri[:, q:q + G], T.su[:, q:q + G]).then_inc(sem("fr", c), 1)
        on_act = split(c)[1]
        ACT.wait_ge(sem("fe", c), G)
        for j in on_act:
            ACT.activation(blk(j), blk(j), Copy, scale=own(c, groups[c].index(j))).then_inc(sem("fg", c), 1)

    def tail(c):
        q = c * G
        runs, on_act = split(c)
        V.wait_ge(sem("fr", c), 1)
        ACT.wait_ge(sem("fg", c), len(on_act))
        ACT.wait_ge(sem("fr", c), 1)
        for run in runs:
            for j in run:
                k = groups[c].index(j)
                if j in on_act:
                    ACT.activation(blk(j), blk(j), Copy, scale=T.ri[:, q + k:q + k + 1]).then_inc(S["sd%d" % j], 1)
                else:
                    V.tensor_scalar(blk(j), blk(j), own(c, k), T.ri[:, q + k:q + k + 1], AluOpType.mult,
                                    AluOpType.mult).then_inc(S["sd%d" % j], 1)
            for j in run:
                SY.wait_ge(S["sd%d" % j], 1)
            lo_c, hi_c = run[0] * NC, (run[-1] + 1) * NC
            SY.dma_start(T.y[:, lo_c:hi_c], T.e[:, lo_c:hi_c]).then_inc(S.st, 16)
            n_st[0] += 16

    c1, c2 = 1 - cls[r], cls[r]
    head(c1)
    sums(c1)
    head(c2)
    tail(c1)
    sums(c2)
    tail(c2)
    SY.wait_ge(S.st, n_st[0])
